import numpy as np
import ml_dtypes


def mxq(x, axis, fmt="e4m3"):
    dtype, down = {"e4m3": (ml_dtypes.float8_e4m3fn, 7), "e5m2": (ml_dtypes.float8_e5m2, 14)}[fmt]
    v = np.moveaxis(np.asarray(x, np.float32).astype(ml_dtypes.bfloat16).astype(np.float64), axis, -1)
    blocks = v.reshape(v.shape[:-1] + (-1, 32))
    amax = np.abs(blocks).max(-1, keepdims=True)
    byte = np.maximum(np.where(amax > 0, np.frexp(amax)[1] - 1 + 127, 0) - down, 1)
    scale = np.exp2(byte - 127.0)
    codes = (blocks / scale).astype(np.float32).astype(dtype).astype(np.float64)
    return np.moveaxis((codes * scale).reshape(v.shape), -1, axis)


WIDE = False


def mx_kscale(k):
    if not WIDE:
        return np.ones(k)
    levels = np.array([10, -10, 5, -5, 0])
    if k % 512:
        return np.exp2(np.random.permutation(np.resize(levels, k // 32))).repeat(32)
    a = np.empty((k // 512, 16))
    for p in range(k // 512):
        a[p, :8] = np.random.permutation(np.resize(levels, 8))
        for g in range(8):
            far = levels[np.abs(levels - a[p, g]) >= 10]
            a[p, g + 8] = far[np.random.randint(len(far))]
    return np.exp2(a.ravel()).repeat(32)


def f64(x):
    return np.asarray(x).astype(np.float64)


def striped(idx):
    return np.tile(idx.reshape(-1, 16).T, (8, 1)).astype(np.uint16)


def unstriped(offs):
    return offs[:16].T.reshape(-1).astype(np.int64)


def striped8(idx):
    return np.concatenate([x.reshape(-1, 16).T for x in idx]).astype(np.uint16)


def runs(offs, k):
    lists = np.stack([offs[16 * r : 16 * r + 16].T.reshape(-1) for r in range(8)]).astype(np.int64)
    return lists[np.arange(k) % 512 // 64]


def pack_weight(w):
    k, n = w.shape
    w = f64(np.asarray(w, np.float32).astype(ml_dtypes.bfloat16)).reshape(k // 32, 32, n)
    amax = np.abs(w).max(1)
    byte = np.clip(np.where(amax > 0, np.frexp(amax)[1] - 1 + 127 - 7, 1), 1, 254)
    scaled = (w * np.exp2(127.0 - byte)[:, None, :]).reshape(k, n).astype(np.float32)
    words = np.ascontiguousarray(scaled.reshape(k // 512, 128, 4, n).transpose(0, 1, 3, 2)).astype(ml_dtypes.float8_e4m3fn).view(np.uint8)
    return words, np.ascontiguousarray(byte.astype(np.uint8).reshape(k // 512, 16, n))


def unpack_weight(words, scales):
    g, p, n, _ = words.shape
    vals = np.ascontiguousarray(words).view(ml_dtypes.float8_e4m3fn).astype(np.float64) * np.repeat(np.exp2(scales.astype(np.float64) - 127.0), 8, axis=1)[..., None]
    return vals.transpose(0, 1, 3, 2).reshape(g * 512, n)


E2M1 = np.array([0.0, 0.5, 1.0, 1.5, 2.0, 3.0, 4.0, 6.0, -0.0, -0.5, -1.0, -1.5, -2.0, -3.0, -4.0, -6.0])


def pack_fp4(w):
    k, n = w.shape
    w = f64(np.asarray(w, np.float32).astype(ml_dtypes.bfloat16)).reshape(k // 32, 32, n)
    amax = np.abs(w).max(1)
    mant, ex = np.frexp(amax / 6.0)
    byte = np.clip(np.where(amax > 0, np.where(mant > 0.5, ex, ex - 1) + 127, 1), 1, 254)
    scaled = (w * np.exp2(127.0 - byte)[:, None, :]).reshape(k, n).astype(np.float32)
    c = np.ascontiguousarray(scaled.reshape(k // 512, 128, 4, n).transpose(0, 1, 3, 2)).astype(ml_dtypes.float4_e2m1fn).view(np.uint8) & 0xF
    words = (c[..., 0::2] | (c[..., 1::2] << 4)).reshape(k // 512, 128, 2 * n)
    return np.ascontiguousarray(words), np.ascontiguousarray(byte.astype(np.uint8).reshape(k // 512, 16, n))


def unpack_fp4(words, scales):
    g, _, n = scales.shape
    words = np.ascontiguousarray(words).reshape(g, 128, n, 2)
    nib = np.empty((g, 128, n, 4), np.uint8)
    nib[..., 0::2] = words & 0xF
    nib[..., 1::2] = words >> 4
    vals = E2M1[nib] * np.repeat(np.exp2(scales.astype(np.float64) - 127.0), 8, axis=1)[..., None]
    return vals.transpose(0, 1, 3, 2).reshape(g * 512, n)


def planes(y):
    n, m = y.shape
    v = y.astype(np.float32).astype(ml_dtypes.bfloat16).astype(np.float64).reshape(n // 32, 32, m)
    top = np.abs(v).max(1)
    byte = np.clip(np.where(top > 0, np.frexp(top)[1] - 1 + 127 - 7, 1), 1, 254)
    codes = (v * np.exp2(127.0 - byte)[:, None, :]).reshape(n, m).astype(np.float32).astype(ml_dtypes.float8_e4m3fn).view(np.uint8)
    words = codes.reshape(n // 512, 128, 4, m).transpose(0, 1, 3, 2)
    return np.ascontiguousarray(words), np.ascontiguousarray(byte.astype(np.uint8).reshape(n // 512, 16, m))


K, T, S, N, H, G = 512, 2048, 512, 512, 512, 2048


def setup_inputs():
    n = np.random.standard_normal
    s = mx_kscale(K)[:, None]
    u = mx_kscale(S)
    packed_xT = pack_weight(n((K, T)) * s)
    packed_w1 = pack_fp4(n((K, H)) / np.sqrt(K) / s)
    packed_w2 = pack_fp4(n((H, N)) / np.sqrt(H) / u[:, None])
    packed_dT = pack_weight(n((K, G)) / s)
    return {
        "x_words": packed_xT[0],
        "x_scales": packed_xT[1],
        "w1_words": packed_w1[0],
        "w1_scales": packed_w1[1],
        "gn": (np.random.uniform(0.5, 1.5, (H, 1)) * u[:, None]).astype(np.float32),
        "w2_words": packed_w2[0],
        "w2_scales": packed_w2[1],
        "d_words": packed_dT[0],
        "d_scales": packed_dT[1],
        "offs": striped(np.random.permutation(T)[:S]),
        "n1": striped8(np.stack([np.random.permutation(S) for _ in range(8)])),
        "n2": striped8(np.stack([np.random.permutation(S) for _ in range(8)])),
        "two": striped(np.random.permutation(T)[:S]),
        "k1": striped8(np.random.randint(0, G, (8, H))),
        "n3": striped8(np.stack([np.random.permutation(S) for _ in range(8)])),
        "n4": striped8(np.stack([np.random.permutation(S) for _ in range(8)])),
    }


def reference(x_words, x_scales, w1_words, w1_scales, gn, w2_words, w2_scales, d_words, d_scales, offs, n1, n2, two, k1, n3, n4):
    xq = unpack_weight(x_words, x_scales)[:, unstriped(offs)]
    y = unpack_fp4(w1_words, w1_scales).T @ xq
    st = np.maximum(y, y[np.arange(H)[:, None], runs(n1, H)])
    z = f64(gn) * (st[np.arange(H)[:, None], runs(n2, H)] - (0.5 * y))
    a = unpack_fp4(w2_words, w2_scales).T @ mxq(z, 0, "e4m3")
    d_k1 = unpack_weight(d_words, d_scales)[np.arange(K)[:, None], runs(k1, K)]
    x_two = unpack_weight(x_words, x_scales)[:, unstriped(two)]
    b = 0.0625 * (d_k1.T @ x_two)
    out_0 = a[np.arange(N)[:, None], runs(n3, N)] - (np.tanh(b) * (b[np.arange(H)[:, None], runs(n4, H)]))
    return (out_0,) + planes(out_0)

@@ -1,0 +1,228 @@
+from contextlib import ExitStack
+
+import concourse.mybir as mybir
+
+F32 = mybir.dt.float32
+BF16 = mybir.dt.bfloat16
+I32 = mybir.dt.int32
+U32 = mybir.dt.uint32
+U16 = mybir.dt.uint16
+U8 = mybir.dt.uint8
+FP8X4 = mybir.dt.float8_e4m3fn_x4
+FP4X4 = mybir.dt.float4_e2m1fn_x4
+ALU = mybir.AluOpType
+ACT = mybir.ActivationFunctionType
+
+P = 128
+PACK = 4
+TABLE = 2048
+S = 512
+HALF = S // 2
+LIST_COLS = S // 16
+
+FLOPS = 3 * 2 * 512 * 512 * 512
+
+
+def tile_picked_cdjoinsoftbhopb_none_po_kernel(
+    tc, x_words, x_scales, w1_words, w1_scales, gn, w2_words, w2_scales, d_words, d_scales,
+    offs, n1, n2, two, k1, n3, n4, out_0, out_1, out_2,
+):
+    nc = tc.nc
+    with ExitStack() as ctx:
+        sb = ctx.enter_context(tc.tile_pool(name="sb", bufs=1))
+        ps = ctx.enter_context(tc.psum_pool(name="ps", bufs=1))
+
+        def tile(shape, dtype, name):
+            return sb.tile(shape, dtype, name=name, align_bytes=64)
+
+        def load_list(src, name):
+            dst = sb.tile([P, LIST_COLS], U16, name=name)
+            nc.sync.dma_start(dst[:], src)
+            return dst
+
+        def half_of(lst, h):
+            return lst[:, h * LIST_COLS // 2 : (h + 1) * LIST_COLS // 2]
+
+        def zeroed_bytes(width, name):
+            dst = tile([P, width], U8, name)
+            nc.vector.memset(dst[:].bitcast(I32), 0)
+            return dst
+
+        def load_scale_rows(queues, dst, src):
+            for q, queue in enumerate(queues):
+                queue.dma_start(dst[32 * q : 32 * q + 4, :].bitcast(I32), src[0, 4 * q : 4 * q + 4, :].bitcast(I32))
+
+        def load_words(dst, src):
+            nc.sync.dma_start(dst[:], src[0].rearrange("p c r -> p (c r)").bitcast(I32))
+
+        def deal(engine, dst, src, per_line, width):
+            engine.tensor_copy(
+                dst[:].rearrange("p (t a i b) -> p a t i b", t=PACK, i=per_line, b=width),
+                src[:].rearrange("p (a i t b) -> p a t i b", t=PACK, i=per_line, b=width),
+            )
+
+        xs_tab = zeroed_bytes(TABLE, "xs_tab")
+        w1s_raw = zeroed_bytes(S, "w1s_raw")
+        ds_tab = zeroed_bytes(TABLE, "ds_tab")
+        w2s_raw = zeroed_bytes(S, "w2s_raw")
+        ds_placed = zeroed_bytes(S, "ds_placed")
+
+        offs_l = load_list(offs, "offs_l")
+        w1w_raw = tile([P, 2 * S], U8, "w1w_raw")
+        nc.scalar.dma_start(w1w_raw[:].bitcast(I32), w1_words[0].bitcast(I32))
+        two_l = load_list(two, "two_l")
+        load_scale_rows([nc.scalar, nc.scalar, nc.sync, nc.scalar], xs_tab, x_scales)
+        xw_tab = tile([P, TABLE], I32, "xw_tab")
+        load_words(xw_tab, x_words)
+        load_scale_rows([nc.scalar] * 4, w1s_raw, w1_scales)
+        n1_l = load_list(n1, "n1_l")
+        k1_l = load_list(k1, "k1_l")
+        for e in range(2):
+            nc.scalar.dma_start(ds_tab[e:P:16, :].bitcast(I32), d_scales[0, e:16:2, :].bitcast(I32))
+        dw_tab = tile([P, TABLE], I32, "dw_tab")
+        load_words(dw_tab, d_words)
+        n2_l = load_list(n2, "n2_l")
+        gain = tile([P, PACK], F32, "gain")
+        nc.sync.dma_start(gain[:], gn.rearrange("(p t) o -> p (t o)", t=PACK))
+        w2w_raw = tile([P, 2 * S], U8, "w2w_raw")
+        nc.sync.dma_start(w2w_raw[:].bitcast(I32), w2_words[0].bitcast(I32))
+        load_scale_rows([nc.gpsimd] * 4, w2s_raw, w2_scales)
+        n4_l = load_list(n4, "n4_l")
+        n3_l = load_list(n3, "n3_l")
+
+        def gather(dst, table, lst):
+            nc.vector.tensor_copy(dst[:], table.indirect(lst[:]))
+
+        w1w = tile([P, 2 * S], U8, "w1w")
+        deal(nc.vector, w1w, w1w_raw, 8, 2)
+        xq_s = tile([P, S], U8, "xq_s")
+        gather(xq_s, xs_tab[:], offs_l)
+        xt_s = tile([P, S], U8, "xt_s")
+        gather(xt_s, xs_tab[:], two_l)
+        w1s = tile([P, S], U8, "w1s")
+        deal(nc.vector, w1s, w1s_raw, 16, 1)
+        xq_w = tile([P, S], U32, "xq_w")
+        gather(xq_w, xw_tab[:].bitcast(U32), offs_l)
+
+        y_ps = [ps.tile([P, S], F32, name="y_ps%d" % t, tag="bank%d" % t) for t in range(PACK)]
+        for t in range(PACK):
+            nc.tensor.matmul_mx(
+                out=y_ps[t][:], lhsT=w1w[:, 2 * P * t : 2 * P * (t + 1)].bitcast(FP4X4), lhsT_scale=w1s[:, P * t : P * (t + 1)],
+                rhs=xq_w[:].bitcast(FP8X4), rhs_scale=xq_s[:], start=True, stop=True,
+            )
+
+        half_y = [tile([P, S], F32, "half_y%d" % t) for t in range(PACK)]
+        near_y = [tile([P, S], F32, "near_y%d" % t) for t in range(PACK)]
+        for t in range(PACK):
+            nc.scalar.activation(half_y[t][:], y_ps[t][:], ACT.Copy, scale=0.5)
+            for h in range(2):
+                nc.scalar.activation(near_y[t][:, h * HALF : (h + 1) * HALF], half_y[t][:].indirect(half_of(n1_l, h)), ACT.Copy)
+
+        dk_s = tile([P, S], U8, "dk_s")
+        gather(dk_s, ds_tab[:], k1_l)
+        dk_s_dealt = tile([P, S], U8, "dk_s_dealt")
+        deal(nc.vector, dk_s_dealt, dk_s, 16, 1)
+        for r in range(4):
+            first = 16 * (r // 2) + r % 2
+            nc.sync.dma_start(ds_placed[r:P:32, :].bitcast(I32), dk_s_dealt[first:P:32, :].bitcast(I32))
+        xt_w = tile([P, S], U32, "xt_w")
+        gather(xt_w, xw_tab[:].bitcast(U32), two_l)
+        dk_w = tile([P, S], U32, "dk_w")
+        gather(dk_w, dw_tab[:].bitcast(U32), k1_l)
+        dk_w_dealt = tile([P, S], U32, "dk_w_dealt")
+        deal(nc.vector, dk_w_dealt, dk_w, 4, 1)
+        w2w = tile([P, 2 * S], U8, "w2w")
+        deal(nc.gpsimd, w2w, w2w_raw, 8, 2)
+        w2s = tile([P, S], U8, "w2s")
+        deal(nc.gpsimd, w2s, w2s_raw, 16, 1)
+
+        b_ps = [ps.tile([P, S], F32, name="b_ps%d" % t, tag="bank%d" % (PACK + t)) for t in range(PACK)]
+        for t in range(PACK):
+            nc.tensor.matmul_mx(
+                out=b_ps[t][:], lhsT=dk_w_dealt[:, P * t : P * (t + 1)].bitcast(FP8X4), lhsT_scale=ds_placed[:, P * t : P * (t + 1)],
+                rhs=xt_w[:].bitcast(FP8X4), rhs_scale=xt_s[:], start=True, stop=True,
+            )
+
+        st = [tile([P, S], F32, "st%d" % t) for t in range(PACK)]
+        diff = [tile([P, PACK, HALF], F32, "diff%d" % h) for h in range(2)]
+        z_bf = [tile([P, PACK * HALF], BF16, "z_bf%d" % h) for h in range(2)]
+        z_w = [tile([P, HALF], U32, "z_w%d" % h) for h in range(2)]
+        z_s = [tile([P, HALF], U8, "z_s%d" % h) for h in range(2)]
+        a_sb = [tile([P, S], F32, "a_sb%d" % t) for t in range(PACK)]
+
+        def make_diff(t, h):
+            nc.vector.tensor_tensor(
+                diff[h][:, t, :], st[t][:].indirect(half_of(n2_l, h)), half_y[t][:, h * HALF : (h + 1) * HALF], ALU.subtract
+            )
+
+        def woven(bf_tile):
+            return bf_tile[:].rearrange("p (c i t) -> p c t i", i=4, t=PACK)
+
+        def planes(f32_tile):
+            return f32_tile[:].rearrange("p t (c i) -> p c t i", i=4)
+
+        def round_z(h):
+            nc.vector.tensor_tensor(
+                woven(z_bf[h]), planes(diff[h]),
+                gain[:].rearrange("p (c t i) -> p c t i", c=1, i=1).to_broadcast([P, HALF // 4, PACK, 4]), ALU.mult,
+            )
+
+        def quantise_z(h):
+            nc.vector.quantize_mx(out=z_w[h][:].bitcast(FP8X4), scales=z_s[h][:], in_=z_bf[h][:])
+
+        def make_a(h):
+            for u in range(2):
+                bank = ps.tile([P, 2, HALF], F32, name="a_ps%d_%d" % (h, u), tag="bank%d" % (2 * h + u))
+                for v in range(2):
+                    t = 2 * u + v
+                    nc.tensor.matmul_mx(
+                        out=bank[:, v, :], lhsT=w2w[:, 2 * P * t : 2 * P * (t + 1)].bitcast(FP4X4), lhsT_scale=w2s[:, P * t : P * (t + 1)],
+                        rhs=z_w[h][:].bitcast(FP8X4), rhs_scale=z_s[h][:], start=True, stop=True,
+                    )
+                for v in range(2):
+                    nc.scalar.copy(a_sb[2 * u + v][:, h * HALF : (h + 1) * HALF], bank[:, v, :])
+
+        for t in range(PACK):
+            nc.vector.scalar_tensor_tensor(st[t][:], near_y[t][:], 2.0, y_ps[t][:], ALU.mult, ALU.max)
+            if t > 0:
+                make_diff(t - 1, 0)
+        make_diff(0, 1)
+        make_diff(PACK - 1, 0)
+        make_diff(1, 1)
+        round_z(0)
+        make_diff(2, 1)
+        quantise_z(0)
+        make_diff(3, 1)
+        make_a(0)
+        round_z(1)
+        quantise_z(1)
+        make_a(1)
+
+        b_sb = [tile([P, S], F32, "b_sb%d" % t) for t in range(PACK)]
+        tanh_b = [tile([P, S], F32, "tanh_b%d" % t) for t in range(PACK)]
+        near_b = [tile([P, S], F32, "near_b%d" % t) for t in range(PACK)]
+        prod = [tile([P, S], F32, "prod%d" % t) for t in range(PACK)]
+        for t in range(PACK):
+            nc.scalar.activation(b_sb[t][:], b_ps[t][:], ACT.Copy, scale=0.0625)
+            nc.scalar.activation(tanh_b[t][:], b_ps[t][:], ACT.Tanh, scale=0.0625)
+            for h in range(2):
+                nc.scalar.activation(near_b[t][:, h * HALF : (h + 1) * HALF], b_sb[t][:].indirect(half_of(n4_l, h)), ACT.Copy)
+            nc.vector.tensor_tensor(prod[t][:], near_b[t][:], tanh_b[t][:], ALU.mult)
+
+        res = [tile([P, PACK, HALF], F32, "res%d" % h) for h in range(2)]
+        o_bf = [tile([P, PACK * HALF], BF16, "o_bf%d" % h) for h in range(2)]
+        o_w = [tile([P, HALF], U32, "o_w%d" % h) for h in range(2)]
+        o_s = tile([P, S], U8, "o_s")
+        out_rows = out_0.rearrange("(p t) c -> p t c", t=PACK)
+        out_words = out_1[0].rearrange("p c r -> p (c r)").bitcast(I32)
+        for h in range(2):
+            cols = slice(h * HALF, (h + 1) * HALF)
+            for t in range(PACK):
+                nc.vector.tensor_tensor(res[h][:, t, :], a_sb[t][:].indirect(half_of(n3_l, h)), prod[t][:, cols], ALU.subtract)
+            nc.sync.dma_start(out_rows[:, :, cols], res[h][:])
+            nc.vector.tensor_copy(woven(o_bf[h]), planes(res[h]))
+            nc.vector.quantize_mx(out=o_w[h][:].bitcast(FP8X4), scales=o_s[:, cols], in_=o_bf[h][:])
+            nc.sync.dma_start(out_words[:, cols], o_w[h][:].bitcast(I32))
+        for q in range(4):
+            queue = nc.sync if q % 2 == 0 else nc.scalar
+            queue.dma_start(out_2[0, 4 * q : 4 * q + 4, :].bitcast(I32), o_s[32 * q : 32 * q + 4, :].bitcast(I32))

@@ -32,8 +32,8 @@ def tile_picked_cdjoinsoftbhopb_none_po_kernel(
         sb = ctx.enter_context(tc.tile_pool(name="sb", bufs=1))
         ps = ctx.enter_context(tc.psum_pool(name="ps", bufs=1))
 
-        def tile(shape, dtype, name):
-            return sb.tile(shape, dtype, name=name, align_bytes=64)
+        def tile(shape, dtype, name, tag=None):
+            return sb.tile(shape, dtype, name=name, tag=tag or name, align_bytes=64)
 
         def load_list(src, name):
             dst = sb.tile([P, LIST_COLS], U16, name=name)
@@ -52,8 +52,8 @@ def tile_picked_cdjoinsoftbhopb_none_po_kernel(
             for q, queue in enumerate(queues):
                 queue.dma_start(dst[32 * q : 32 * q + 4, :].bitcast(I32), src[0, 4 * q : 4 * q + 4, :].bitcast(I32))
 
-        def load_words(dst, src):
-            nc.sync.dma_start(dst[:], src[0].rearrange("p c r -> p (c r)").bitcast(I32))
+        def load_words(queue, dst, src):
+            queue.dma_start(dst[:], src[0].rearrange("p c r -> p (c r)").bitcast(I32))
 
         def deal(engine, dst, src, per_line, width):
             engine.tensor_copy(
@@ -71,36 +71,28 @@ def tile_picked_cdjoinsoftbhopb_none_po_kernel(
         w1w_raw = tile([P, 2 * S], U8, "w1w_raw")
         nc.scalar.dma_start(w1w_raw[:].bitcast(I32), w1_words[0].bitcast(I32))
         two_l = load_list(two, "two_l")
-        load_scale_rows([nc.scalar, nc.scalar, nc.sync, nc.scalar], xs_tab, x_scales)
+        load_scale_rows([nc.sync, nc.sync, nc.scalar, nc.scalar], xs_tab, x_scales)
         xw_tab = tile([P, TABLE], I32, "xw_tab")
-        load_words(xw_tab, x_words)
-        load_scale_rows([nc.scalar] * 4, w1s_raw, w1_scales)
-        n1_l = load_list(n1, "n1_l")
+        load_words(nc.sync, xw_tab, x_words)
+        load_scale_rows([nc.sync] * 4, w1s_raw, w1_scales)
         k1_l = load_list(k1, "k1_l")
-        for e in range(2):
-            nc.scalar.dma_start(ds_tab[e:P:16, :].bitcast(I32), d_scales[0, e:16:2, :].bitcast(I32))
-        dw_tab = tile([P, TABLE], I32, "dw_tab")
-        load_words(dw_tab, d_words)
+        nc.sync.dma_start(ds_tab[0:P:8, :].bitcast(I32), d_scales[0].bitcast(I32))
+        n1_l = load_list(n1, "n1_l")
         n2_l = load_list(n2, "n2_l")
-        gain = tile([P, PACK], F32, "gain")
-        nc.sync.dma_start(gain[:], gn.rearrange("(p t) o -> p (t o)", t=PACK))
-        w2w_raw = tile([P, 2 * S], U8, "w2w_raw")
-        nc.sync.dma_start(w2w_raw[:].bitcast(I32), w2_words[0].bitcast(I32))
-        load_scale_rows([nc.gpsimd] * 4, w2s_raw, w2_scales)
-        n4_l = load_list(n4, "n4_l")
-        n3_l = load_list(n3, "n3_l")
 
         def gather(dst, table, lst):
             nc.vector.tensor_copy(dst[:], table.indirect(lst[:]))
 
         w1w = tile([P, 2 * S], U8, "w1w")
-        deal(nc.vector, w1w, w1w_raw, 8, 2)
+        deal(nc.gpsimd, w1w, w1w_raw, 8, 2)
+        dw_tab = tile([P, TABLE], I32, "dw_tab", "w1w_raw")
+        load_words(nc.scalar, dw_tab, d_words)
         xq_s = tile([P, S], U8, "xq_s")
         gather(xq_s, xs_tab[:], offs_l)
         xt_s = tile([P, S], U8, "xt_s")
         gather(xt_s, xs_tab[:], two_l)
         w1s = tile([P, S], U8, "w1s")
-        deal(nc.vector, w1s, w1s_raw, 16, 1)
+        deal(nc.gpsimd, w1s, w1s_raw, 16, 1)
         xq_w = tile([P, S], U32, "xq_w")
         gather(xq_w, xw_tab[:].bitcast(U32), offs_l)
 
@@ -123,11 +115,17 @@ def tile_picked_cdjoinsoftbhopb_none_po_kernel(
         dk_s_dealt = tile([P, S], U8, "dk_s_dealt")
         deal(nc.vector, dk_s_dealt, dk_s, 16, 1)
         for r in range(4):
-            first = 16 * (r // 2) + r % 2
-            nc.sync.dma_start(ds_placed[r:P:32, :].bitcast(I32), dk_s_dealt[first:P:32, :].bitcast(I32))
+            nc.sync.dma_start(ds_placed[r:P:32, :].bitcast(I32), dk_s_dealt[8 * r : P : 32, :].bitcast(I32))
+        gain = tile([P, PACK], F32, "gain")
+        nc.sync.dma_start(gain[:], gn.rearrange("(p t) o -> p (t o)", t=PACK))
+        n4_l = load_list(n4, "n4_l")
+        w2w_raw = tile([P, 2 * S], U8, "w2w_raw")
+        nc.sync.dma_start(w2w_raw[:].bitcast(I32), w2_words[0].bitcast(I32))
+        load_scale_rows([nc.sync] * 4, w2s_raw, w2_scales)
+        n3_l = load_list(n3, "n3_l")
         xt_w = tile([P, S], U32, "xt_w")
         gather(xt_w, xw_tab[:].bitcast(U32), two_l)
-        dk_w = tile([P, S], U32, "dk_w")
+        dk_w = tile([P, S], U32, "dk_w", "dk_s")
         gather(dk_w, dw_tab[:].bitcast(U32), k1_l)
         dk_w_dealt = tile([P, S], U32, "dk_w_dealt")
         deal(nc.vector, dk_w_dealt, dk_w, 4, 1)
@@ -143,7 +141,7 @@ def tile_picked_cdjoinsoftbhopb_none_po_kernel(
                 rhs=xt_w[:].bitcast(FP8X4), rhs_scale=xt_s[:], start=True, stop=True,
             )
 
-        st = [tile([P, S], F32, "st%d" % t) for t in range(PACK)]
+        st = [tile([P, S], F32, "st%d" % t, "dk_s" if t == 0 else None) for t in range(PACK)]
         diff = [tile([P, PACK, HALF], F32, "diff%d" % h) for h in range(2)]
         z_bf = [tile([P, PACK * HALF], BF16, "z_bf%d" % h) for h in range(2)]
         z_w = [tile([P, HALF], U32, "z_w%d" % h) for h in range(2)]
@@ -198,8 +196,8 @@ def tile_picked_cdjoinsoftbhopb_none_po_kernel(
         quantise_z(1)
         make_a(1)
 
-        b_sb = [tile([P, S], F32, "b_sb%d" % t) for t in range(PACK)]
-        tanh_b = [tile([P, S], F32, "tanh_b%d" % t) for t in range(PACK)]
+        b_sb = [tile([P, S], F32, "b_sb%d" % t, "z_w1" if t == PACK - 1 else None) for t in range(PACK)]
+        tanh_b = [tile([P, S], F32, "tanh_b%d" % t, "z_s1" if t == PACK - 1 else None) for t in range(PACK)]
         near_b = [tile([P, S], F32, "near_b%d" % t) for t in range(PACK)]
         prod = [tile([P, S], F32, "prod%d" % t) for t in range(PACK)]
         for t in range(PACK):
@@ -215,14 +213,22 @@ def tile_picked_cdjoinsoftbhopb_none_po_kernel(
         o_s = tile([P, S], U8, "o_s")
         out_rows = out_0.rearrange("(p t) c -> p t c", t=PACK)
         out_words = out_1[0].rearrange("p c r -> p (c r)").bitcast(I32)
+        near_a = tile([P, S], F32, "near_a")
         for h in range(2):
             cols = slice(h * HALF, (h + 1) * HALF)
             for t in range(PACK):
-                nc.vector.tensor_tensor(res[h][:, t, :], a_sb[t][:].indirect(half_of(n3_l, h)), prod[t][:, cols], ALU.subtract)
-            nc.sync.dma_start(out_rows[:, :, cols], res[h][:])
-            nc.vector.tensor_copy(woven(o_bf[h]), planes(res[h]))
+                if t < PACK - 1:
+                    nc.vector.tensor_tensor(res[h][:, t, :], a_sb[t][:].indirect(half_of(n3_l, h)), prod[t][:, cols], ALU.subtract)
+                else:
+                    nc.scalar.activation(near_a[:, cols], a_sb[t][:].indirect(half_of(n3_l, h)), ACT.Copy)
+                    nc.vector.tensor_tensor(res[h][:, t, :], near_a[:, cols], prod[t][:, cols], ALU.subtract)
+                nc.sync.dma_start(out_rows[:, t, cols], res[h][:, t, :])
+        nc.scalar.copy(woven(o_bf[0]), planes(res[0]))
+        nc.vector.tensor_copy(woven(o_bf[1]), planes(res[1]))
+        for h in (1, 0):
+            cols = slice(h * HALF, (h + 1) * HALF)
             nc.vector.quantize_mx(out=o_w[h][:].bitcast(FP8X4), scales=o_s[:, cols], in_=o_bf[h][:])
             nc.sync.dma_start(out_words[:, cols], o_w[h][:].bitcast(I32))
         for q in range(4):
-            queue = nc.sync if q % 2 == 0 else nc.scalar
+            queue = nc.scalar if q % 2 == 0 else nc.sync
             queue.dma_start(out_2[0, 4 * q : 4 * q + 4, :].bitcast(I32), o_s[32 * q : 32 * q + 4, :].bitcast(I32))

@@ -61,7 +61,9 @@ def tile_picked_cdjoinsoftbhopb_none_po_kernel(
                 src[:].rearrange("p (a i t b) -> p a t i b", t=PACK, i=per_line, b=width),
             )
 
-        xs_tab = zeroed_bytes(TABLE, "xs_tab")
+        xs_tab = tile([P, TABLE], U8, "xs_tab")
+        nc.vector.memset(xs_tab[:, : TABLE // 2].bitcast(I32), 0)
+        nc.gpsimd.memset(xs_tab[:, TABLE // 2 :].bitcast(I32), 0)
         w1s_raw = zeroed_bytes(S, "w1s_raw")
         ds_tab = zeroed_bytes(TABLE, "ds_tab")
         w2s_raw = zeroed_bytes(S, "w2s_raw")
@@ -104,11 +106,11 @@ def tile_picked_cdjoinsoftbhopb_none_po_kernel(
             )
 
         half_y = [tile([P, S], F32, "half_y%d" % t) for t in range(PACK)]
-        near_y = [tile([P, S], F32, "near_y%d" % t) for t in range(PACK)]
+        st = [tile([P, 2 * S], F32, "st%d" % t) for t in range(PACK)]
         for t in range(PACK):
             nc.scalar.activation(half_y[t][:], y_ps[t][:], ACT.Copy, scale=0.5)
             for h in range(2):
-                nc.scalar.activation(near_y[t][:, h * HALF : (h + 1) * HALF], half_y[t][:].indirect(half_of(n1_l, h)), ACT.Copy)
+                nc.scalar.activation(st[t][:, S + h * HALF : S + (h + 1) * HALF], half_y[t][:].indirect(half_of(n1_l, h)), ACT.Copy)
 
         dk_s = tile([P, S], U8, "dk_s")
         gather(dk_s, ds_tab[:], k1_l)
@@ -141,71 +143,57 @@ def tile_picked_cdjoinsoftbhopb_none_po_kernel(
                 rhs=xt_w[:].bitcast(FP8X4), rhs_scale=xt_s[:], start=True, stop=True,
             )
 
-        st = [tile([P, S], F32, "st%d" % t, "dk_s" if t == 0 else None) for t in range(PACK)]
-        diff = [tile([P, PACK, HALF], F32, "diff%d" % h) for h in range(2)]
+        diff = tile([P, PACK, S], F32, "diff", "dk_s")
         z_bf = [tile([P, PACK * HALF], BF16, "z_bf%d" % h) for h in range(2)]
-        z_w = [tile([P, HALF], U32, "z_w%d" % h) for h in range(2)]
-        z_s = [tile([P, HALF], U8, "z_s%d" % h) for h in range(2)]
-        a_sb = [tile([P, S], F32, "a_sb%d" % t) for t in range(PACK)]
+        z_w = tile([P, S], U32, "z_w")
+        z_s = tile([P, S], U8, "z_s")
 
-        def make_diff(t, h):
-            nc.vector.tensor_tensor(
-                diff[h][:, t, :], st[t][:].indirect(half_of(n2_l, h)), half_y[t][:, h * HALF : (h + 1) * HALF], ALU.subtract
-            )
+        def cols(h):
+            return slice(h * HALF, (h + 1) * HALF)
 
         def woven(bf_tile):
             return bf_tile[:].rearrange("p (c i t) -> p c t i", i=4, t=PACK)
 
-        def planes(f32_tile):
-            return f32_tile[:].rearrange("p t (c i) -> p c t i", i=4)
+        def planes(f32_ap):
+            return f32_ap.rearrange("p t (c i) -> p c t i", i=4)
 
         def round_z(h):
             nc.vector.tensor_tensor(
-                woven(z_bf[h]), planes(diff[h]),
+                woven(z_bf[h]), planes(diff[:, :, cols(h)]),
                 gain[:].rearrange("p (c t i) -> p c t i", c=1, i=1).to_broadcast([P, HALF // 4, PACK, 4]), ALU.mult,
             )
 
-        def quantise_z(h):
-            nc.vector.quantize_mx(out=z_w[h][:].bitcast(FP8X4), scales=z_s[h][:], in_=z_bf[h][:])
-
-        def make_a(h):
-            for u in range(2):
-                bank = ps.tile([P, 2, HALF], F32, name="a_ps%d_%d" % (h, u), tag="bank%d" % (2 * h + u))
-                for v in range(2):
-                    t = 2 * u + v
-                    nc.tensor.matmul_mx(
-                        out=bank[:, v, :], lhsT=w2w[:, 2 * P * t : 2 * P * (t + 1)].bitcast(FP4X4), lhsT_scale=w2s[:, P * t : P * (t + 1)],
-                        rhs=z_w[h][:].bitcast(FP8X4), rhs_scale=z_s[h][:], start=True, stop=True,
-                    )
-                for v in range(2):
-                    nc.scalar.copy(a_sb[2 * u + v][:, h * HALF : (h + 1) * HALF], bank[:, v, :])
-
         for t in range(PACK):
-            nc.vector.scalar_tensor_tensor(st[t][:], near_y[t][:], 2.0, y_ps[t][:], ALU.mult, ALU.max)
-            if t > 0:
-                make_diff(t - 1, 0)
-        make_diff(0, 1)
-        make_diff(PACK - 1, 0)
-        make_diff(1, 1)
-        round_z(0)
-        make_diff(2, 1)
-        quantise_z(0)
-        make_diff(3, 1)
-        make_a(0)
-        round_z(1)
-        quantise_z(1)
-        make_a(1)
+            nc.vector.scalar_tensor_tensor(st[t][:, :S], st[t][:, S:], 2.0, y_ps[t][:], ALU.mult, ALU.max)
+            nc.vector.tensor_tensor(diff[:, t, :], st[t][:].indirect(n2_l[:]), half_y[t][:], ALU.subtract)
+        for h in range(2):
+            round_z(h)
+        for h in range(2):
+            nc.vector.quantize_mx(out=z_w[:, cols(h)].bitcast(FP8X4), scales=z_s[:, cols(h)], in_=z_bf[h][:])
 
-        b_sb = [tile([P, S], F32, "b_sb%d" % t, "z_w1" if t == PACK - 1 else None) for t in range(PACK)]
-        tanh_b = [tile([P, S], F32, "tanh_b%d" % t, "z_s1" if t == PACK - 1 else None) for t in range(PACK)]
-        near_b = [tile([P, S], F32, "near_b%d" % t) for t in range(PACK)]
+        b_sb = [tile([P, S], F32, "b_sb%d" % t) for t in range(PACK)]
+        tanh_b = [tile([P, S], F32, "tanh_b%d" % t) for t in range(PACK)]
         prod = [tile([P, S], F32, "prod%d" % t) for t in range(PACK)]
         for t in range(PACK):
             nc.scalar.activation(b_sb[t][:], b_ps[t][:], ACT.Copy, scale=0.0625)
             nc.scalar.activation(tanh_b[t][:], b_ps[t][:], ACT.Tanh, scale=0.0625)
-            for h in range(2):
-                nc.scalar.activation(near_b[t][:, h * HALF : (h + 1) * HALF], b_sb[t][:].indirect(half_of(n4_l, h)), ACT.Copy)
-            nc.vector.tensor_tensor(prod[t][:], near_b[t][:], tanh_b[t][:], ALU.mult)
+            if t < PACK - 1:
+                near_b = tile([P, S], F32, "near_b%d" % t)
+                for h in range(2):
+                    nc.scalar.activation(near_b[:, cols(h)], b_sb[t][:].indirect(half_of(n4_l, h)), ACT.Copy)
+                nc.vector.tensor_tensor(prod[t][:], near_b[:], tanh_b[t][:], ALU.mult)
+            else:
+                for h in range(2):
+                    nc.vector.tensor_tensor(prod[t][:, cols(h)], b_sb[t][:].indirect(half_of(n4_l, h)), tanh_b[t][:, cols(h)], ALU.mult)
+
+        a_sb = [tile([P, S], F32, "a_sb%d" % t) for t in range(PACK)]
+        for t in range(PACK):
+            a_ps = ps.tile([P, S], F32, name="a_ps%d" % t, tag="bank%d" % t)
+            nc.tensor.matmul_mx(
+                out=a_ps[:], lhsT=w2w[:, 2 * P * t : 2 * P * (t + 1)].bitcast(FP4X4), lhsT_scale=w2s[:, P * t : P * (t + 1)],
+                rhs=z_w[:].bitcast(FP8X4), rhs_scale=z_s[:], start=True, stop=True,
+            )
+            nc.scalar.copy(a_sb[t][:], a_ps[:])
 
         res = [tile([P, PACK, HALF], F32, "res%d" % h) for h in range(2)]
         o_bf = [tile([P, PACK * HALF], BF16, "o_bf%d" % h) for h in range(2)]
@@ -213,22 +201,20 @@ def tile_picked_cdjoinsoftbhopb_none_po_kernel(
         o_s = tile([P, S], U8, "o_s")
         out_rows = out_0.rearrange("(p t) c -> p t c", t=PACK)
         out_words = out_1[0].rearrange("p c r -> p (c r)").bitcast(I32)
-        near_a = tile([P, S], F32, "near_a")
+        near_a = tile([P, PACK, HALF], F32, "near_a")
+        for t in range(PACK):
+            nc.scalar.activation(near_a[:, t, :], a_sb[t][:].indirect(half_of(n3_l, 1)), ACT.Copy)
+            nc.vector.tensor_tensor(res[0][:, t, :], a_sb[t][:].indirect(half_of(n3_l, 0)), prod[t][:, cols(0)], ALU.subtract)
+        nc.sync.dma_start(out_rows[:, :, cols(0)], res[0][:])
+        nc.scalar.copy(woven(o_bf[0]), planes(res[0][:]))
+        for t in range(PACK):
+            nc.vector.tensor_tensor(res[1][:, t, :], near_a[:, t, :], prod[t][:, cols(1)], ALU.subtract)
+            if t % 2 == 1:
+                nc.sync.dma_start(out_rows[:, t - 1 : t + 1, cols(1)], res[1][:, t - 1 : t + 1, :])
+        nc.vector.tensor_copy(woven(o_bf[1]), planes(res[1][:]))
         for h in range(2):
-            cols = slice(h * HALF, (h + 1) * HALF)
-            for t in range(PACK):
-                if t < PACK - 1:
-                    nc.vector.tensor_tensor(res[h][:, t, :], a_sb[t][:].indirect(half_of(n3_l, h)), prod[t][:, cols], ALU.subtract)
-                else:
-                    nc.scalar.activation(near_a[:, cols], a_sb[t][:].indirect(half_of(n3_l, h)), ACT.Copy)
-                    nc.vector.tensor_tensor(res[h][:, t, :], near_a[:, cols], prod[t][:, cols], ALU.subtract)
-                nc.sync.dma_start(out_rows[:, t, cols], res[h][:, t, :])
-        nc.scalar.copy(woven(o_bf[0]), planes(res[0]))
-        nc.vector.tensor_copy(woven(o_bf[1]), planes(res[1]))
-        for h in (1, 0):
-            cols = slice(h * HALF, (h + 1) * HALF)
-            nc.vector.quantize_mx(out=o_w[h][:].bitcast(FP8X4), scales=o_s[:, cols], in_=o_bf[h][:])
-            nc.sync.dma_start(out_words[:, cols], o_w[h][:].bitcast(I32))
+            nc.vector.quantize_mx(out=o_w[h][:].bitcast(FP8X4), scales=o_s[:, cols(h)], in_=o_bf[h][:])
+            nc.sync.dma_start(out_words[:, cols(h)], o_w[h][:].bitcast(I32))
         for q in range(4):
             queue = nc.scalar if q % 2 == 0 else nc.sync
             queue.dma_start(out_2[0, 4 * q : 4 * q + 4, :].bitcast(I32), o_s[32 * q : 32 * q + 4, :].bitcast(I32))

from contextlib import ExitStack

import concourse.mybir as mybir

F32 = mybir.dt.float32
BF16 = mybir.dt.bfloat16
I32 = mybir.dt.int32
U32 = mybir.dt.uint32
U16 = mybir.dt.uint16
U8 = mybir.dt.uint8
FP8X4 = mybir.dt.float8_e4m3fn_x4
FP4X4 = mybir.dt.float4_e2m1fn_x4
ALU = mybir.AluOpType
ACT = mybir.ActivationFunctionType

P = 128
PACK = 4
TABLE = 2048
S = 512
HALF = S // 2
LIST_COLS = S // 16

FLOPS = 3 * 2 * 512 * 512 * 512


def tile_picked_cdjoinsoftbhopb_none_po_kernel(
    tc, x_words, x_scales, w1_words, w1_scales, gn, w2_words, w2_scales, d_words, d_scales,
    offs, n1, n2, two, k1, n3, n4, out_0, out_1, out_2,
):
    nc = tc.nc
    with ExitStack() as ctx:
        sb = ctx.enter_context(tc.tile_pool(name="sb", bufs=1))
        ps = ctx.enter_context(tc.psum_pool(name="ps", bufs=1))

        def tile(shape, dtype, name, tag=None):
            return sb.tile(shape, dtype, name=name, tag=tag or name, align_bytes=64)

        def load_list(src, name):
            dst = sb.tile([P, LIST_COLS], U16, name=name)
            nc.sync.dma_start(dst[:], src)
            return dst

        def half_of(lst, h):
            return lst[:, h * LIST_COLS // 2 : (h + 1) * LIST_COLS // 2]

        def zeroed_bytes(width, name):
            dst = tile([P, width], U8, name)
            nc.vector.memset(dst[:].bitcast(I32), 0)
            return dst

        def load_scale_rows(queues, dst, src):
            for q, queue in enumerate(queues):
                queue.dma_start(dst[32 * q : 32 * q + 4, :].bitcast(I32), src[0, 4 * q : 4 * q + 4, :].bitcast(I32))

        def load_words(queue, dst, src):
            queue.dma_start(dst[:], src[0].rearrange("p c r -> p (c r)").bitcast(I32))

        def deal(engine, dst, src, per_line, width):
            engine.tensor_copy(
                dst[:].rearrange("p (t a i b) -> p a t i b", t=PACK, i=per_line, b=width),
                src[:].rearrange("p (a i t b) -> p a t i b", t=PACK, i=per_line, b=width),
            )

        xs_tab = tile([P, TABLE], U8, "xs_tab")
        nc.vector.memset(xs_tab[:, : TABLE // 2].bitcast(I32), 0)
        nc.gpsimd.memset(xs_tab[:, TABLE // 2 :].bitcast(I32), 0)
        w1s_raw = zeroed_bytes(S, "w1s_raw")
        ds_tab = zeroed_bytes(TABLE, "ds_tab")
        w2s_raw = zeroed_bytes(S, "w2s_raw")
        ds_placed = zeroed_bytes(S, "ds_placed")

        offs_l = load_list(offs, "offs_l")
        w1w_raw = tile([P, 2 * S], U8, "w1w_raw")
        nc.scalar.dma_start(w1w_raw[:].bitcast(I32), w1_words[0].bitcast(I32))
        two_l = load_list(two, "two_l")
        load_scale_rows([nc.sync, nc.sync, nc.scalar, nc.scalar], xs_tab, x_scales)
        xw_tab = tile([P, TABLE], I32, "xw_tab")
        load_words(nc.sync, xw_tab, x_words)
        load_scale_rows([nc.sync] * 4, w1s_raw, w1_scales)
        k1_l = load_list(k1, "k1_l")
        nc.sync.dma_start(ds_tab[0:P:8, :].bitcast(I32), d_scales[0].bitcast(I32))
        n1_l = load_list(n1, "n1_l")
        n2_l = load_list(n2, "n2_l")

        def gather(dst, table, lst):
            nc.vector.tensor_copy(dst[:], table.indirect(lst[:]))

        w1w = tile([P, 2 * S], U8, "w1w")
        deal(nc.gpsimd, w1w, w1w_raw, 8, 2)
        dw_tab = tile([P, TABLE], I32, "dw_tab", "w1w_raw")
        load_words(nc.scalar, dw_tab, d_words)
        xq_s = tile([P, S], U8, "xq_s")
        gather(xq_s, xs_tab[:], offs_l)
        xt_s = tile([P, S], U8, "xt_s")
        gather(xt_s, xs_tab[:], two_l)
        w1s = tile([P, S], U8, "w1s")
        deal(nc.gpsimd, w1s, w1s_raw, 16, 1)
        xq_w = tile([P, S], U32, "xq_w")
        gather(xq_w, xw_tab[:].bitcast(U32), offs_l)

        y_ps = [ps.tile([P, S], F32, name="y_ps%d" % t, tag="bank%d" % t) for t in range(PACK)]
        for t in range(PACK):
            nc.tensor.matmul_mx(
                out=y_ps[t][:], lhsT=w1w[:, 2 * P * t : 2 * P * (t + 1)].bitcast(FP4X4), lhsT_scale=w1s[:, P * t : P * (t + 1)],
                rhs=xq_w[:].bitcast(FP8X4), rhs_scale=xq_s[:], start=True, stop=True,
            )

        half_y = [tile([P, S], F32, "half_y%d" % t) for t in range(PACK)]
        st = [tile([P, 2 * S], F32, "st%d" % t) for t in range(PACK)]
        for t in range(PACK):
            nc.scalar.activation(half_y[t][:], y_ps[t][:], ACT.Copy, scale=0.5)
            for h in range(2):
                nc.scalar.activation(st[t][:, S + h * HALF : S + (h + 1) * HALF], half_y[t][:].indirect(half_of(n1_l, h)), ACT.Copy)

        dk_s = tile([P, S], U8, "dk_s")
        gather(dk_s, ds_tab[:], k1_l)
        dk_s_dealt = tile([P, S], U8, "dk_s_dealt")
        deal(nc.vector, dk_s_dealt, dk_s, 16, 1)
        for r in range(4):
            nc.sync.dma_start(ds_placed[r:P:32, :].bitcast(I32), dk_s_dealt[8 * r : P : 32, :].bitcast(I32))
        gain = tile([P, PACK], F32, "gain")
        nc.sync.dma_start(gain[:], gn.rearrange("(p t) o -> p (t o)", t=PACK))
        n4_l = load_list(n4, "n4_l")
        w2w_raw = tile([P, 2 * S], U8, "w2w_raw")
        nc.sync.dma_start(w2w_raw[:].bitcast(I32), w2_words[0].bitcast(I32))
        load_scale_rows([nc.sync] * 4, w2s_raw, w2_scales)
        n3_l = load_list(n3, "n3_l")
        xt_w = tile([P, S], U32, "xt_w")
        gather(xt_w, xw_tab[:].bitcast(U32), two_l)
        dk_w = tile([P, S], U32, "dk_w", "dk_s")
        gather(dk_w, dw_tab[:].bitcast(U32), k1_l)
        dk_w_dealt = tile([P, S], U32, "dk_w_dealt")
        deal(nc.vector, dk_w_dealt, dk_w, 4, 1)
        w2w = tile([P, 2 * S], U8, "w2w")
        deal(nc.gpsimd, w2w, w2w_raw, 8, 2)
        w2s = tile([P, S], U8, "w2s")
        deal(nc.gpsimd, w2s, w2s_raw, 16, 1)

        b_ps = [ps.tile([P, S], F32, name="b_ps%d" % t, tag="bank%d" % (PACK + t)) for t in range(PACK)]
        for t in range(PACK):
            nc.tensor.matmul_mx(
                out=b_ps[t][:], lhsT=dk_w_dealt[:, P * t : P * (t + 1)].bitcast(FP8X4), lhsT_scale=ds_placed[:, P * t : P * (t + 1)],
                rhs=xt_w[:].bitcast(FP8X4), rhs_scale=xt_s[:], start=True, stop=True,
            )

        diff = tile([P, PACK, S], F32, "diff", "dk_s")
        z_bf = [tile([P, PACK * HALF], BF16, "z_bf%d" % h) for h in range(2)]
        z_w = tile([P, S], U32, "z_w")
        z_s = tile([P, S], U8, "z_s")

        def cols(h):
            return slice(h * HALF, (h + 1) * HALF)

        def woven(bf_tile):
            return bf_tile[:].rearrange("p (c i t) -> p c t i", i=4, t=PACK)

        def planes(f32_ap):
            return f32_ap.rearrange("p t (c i) -> p c t i", i=4)

        def round_z(h):
            nc.vector.tensor_tensor(
                woven(z_bf[h]), planes(diff[:, :, cols(h)]),
                gain[:].rearrange("p (c t i) -> p c t i", c=1, i=1).to_broadcast([P, HALF // 4, PACK, 4]), ALU.mult,
            )

        for t in range(PACK):
            nc.vector.scalar_tensor_tensor(st[t][:, :S], st[t][:, S:], 2.0, y_ps[t][:], ALU.mult, ALU.max)
            nc.vector.tensor_tensor(diff[:, t, :], st[t][:].indirect(n2_l[:]), half_y[t][:], ALU.subtract)
        for h in range(2):
            round_z(h)
        for h in range(2):
            nc.vector.quantize_mx(out=z_w[:, cols(h)].bitcast(FP8X4), scales=z_s[:, cols(h)], in_=z_bf[h][:])

        b_sb = [tile([P, S], F32, "b_sb%d" % t) for t in range(PACK)]
        tanh_b = [tile([P, S], F32, "tanh_b%d" % t) for t in range(PACK)]
        prod = [tile([P, S], F32, "prod%d" % t) for t in range(PACK)]
        for t in range(PACK):
            nc.scalar.activation(b_sb[t][:], b_ps[t][:], ACT.Copy, scale=0.0625)
            nc.scalar.activation(tanh_b[t][:], b_ps[t][:], ACT.Tanh, scale=0.0625)
            if t < PACK - 1:
                near_b = tile([P, S], F32, "near_b%d" % t)
                for h in range(2):
                    nc.scalar.activation(near_b[:, cols(h)], b_sb[t][:].indirect(half_of(n4_l, h)), ACT.Copy)
                nc.vector.tensor_tensor(prod[t][:], near_b[:], tanh_b[t][:], ALU.mult)
            else:
                for h in range(2):
                    nc.vector.tensor_tensor(prod[t][:, cols(h)], b_sb[t][:].indirect(half_of(n4_l, h)), tanh_b[t][:, cols(h)], ALU.mult)

        a_sb = [tile([P, S], F32, "a_sb%d" % t) for t in range(PACK)]
        for t in range(PACK):
            a_ps = ps.tile([P, S], F32, name="a_ps%d" % t, tag="bank%d" % t)
            nc.tensor.matmul_mx(
                out=a_ps[:], lhsT=w2w[:, 2 * P * t : 2 * P * (t + 1)].bitcast(FP4X4), lhsT_scale=w2s[:, P * t : P * (t + 1)],
                rhs=z_w[:].bitcast(FP8X4), rhs_scale=z_s[:], start=True, stop=True,
            )
            nc.scalar.copy(a_sb[t][:], a_ps[:])

        res = [tile([P, PACK, HALF], F32, "res%d" % h) for h in range(2)]
        o_bf = [tile([P, PACK * HALF], BF16, "o_bf%d" % h) for h in range(2)]
        o_w = [tile([P, HALF], U32, "o_w%d" % h) for h in range(2)]
        o_s = tile([P, S], U8, "o_s")
        out_rows = out_0.rearrange("(p t) c -> p t c", t=PACK)
        out_words = out_1[0].rearrange("p c r -> p (c r)").bitcast(I32)
        near_a = tile([P, PACK, HALF], F32, "near_a")
        for t in range(PACK):
            nc.scalar.activation(near_a[:, t, :], a_sb[t][:].indirect(half_of(n3_l, 1)), ACT.Copy)
            nc.vector.tensor_tensor(res[0][:, t, :], a_sb[t][:].indirect(half_of(n3_l, 0)), prod[t][:, cols(0)], ALU.subtract)
        nc.sync.dma_start(out_rows[:, :, cols(0)], res[0][:])
        nc.scalar.copy(woven(o_bf[0]), planes(res[0][:]))
        for t in range(PACK):
            nc.vector.tensor_tensor(res[1][:, t, :], near_a[:, t, :], prod[t][:, cols(1)], ALU.subtract)
            if t % 2 == 1:
                nc.sync.dma_start(out_rows[:, t - 1 : t + 1, cols(1)], res[1][:, t - 1 : t + 1, :])
        nc.vector.tensor_copy(woven(o_bf[1]), planes(res[1][:]))
        for h in range(2):
            nc.vector.quantize_mx(out=o_w[h][:].bitcast(FP8X4), scales=o_s[:, cols(h)], in_=o_bf[h][:])
            nc.sync.dma_start(out_words[:, cols(h)], o_w[h][:].bitcast(I32))
        for q in range(4):
            queue = nc.scalar if q % 2 == 0 else nc.sync
            queue.dma_start(out_2[0, 4 * q : 4 * q + 4, :].bitcast(I32), o_s[32 * q : 32 * q + 4, :].bitcast(I32))
